import numpy as np
import ml_dtypes


def mxq(x, axis, fmt="e4m3"):
    dtype, down = {"e4m3": (ml_dtypes.float8_e4m3fn, 7), "e5m2": (ml_dtypes.float8_e5m2, 14)}[fmt]
    v = np.moveaxis(np.asarray(x, np.float32).astype(ml_dtypes.bfloat16).astype(np.float64), axis, -1)
    blocks = v.reshape(v.shape[:-1] + (-1, 32))
    amax = np.abs(blocks).max(-1, keepdims=True)
    byte = np.maximum(np.where(amax > 0, np.frexp(amax)[1] - 1 + 127, 0) - down, 1)
    scale = np.exp2(byte - 127.0)
    codes = (blocks / scale).astype(np.float32).astype(dtype).astype(np.float64)
    return np.moveaxis((codes * scale).reshape(v.shape), -1, axis)


WIDE = False


def mx_kscale(k):
    if not WIDE:
        return np.ones(k)
    levels = np.array([10, -10, 5, -5, 0])
    if k % 512:
        return np.exp2(np.random.permutation(np.resize(levels, k // 32))).repeat(32)
    a = np.empty((k // 512, 16))
    for p in range(k // 512):
        a[p, :8] = np.random.permutation(np.resize(levels, 8))
        for g in range(8):
            far = levels[np.abs(levels - a[p, g]) >= 10]
            a[p, g + 8] = far[np.random.randint(len(far))]
    return np.exp2(a.ravel()).repeat(32)


def f64(x):
    return np.asarray(x).astype(np.float64)


def striped(idx):
    return np.tile(idx.reshape(-1, 16).T, (8, 1)).astype(np.uint16)


def unstriped(offs):
    return offs[:16].T.reshape(-1).astype(np.int64)


E2M1 = np.array([0.0, 0.5, 1.0, 1.5, 2.0, 3.0, 4.0, 6.0, -0.0, -0.5, -1.0, -1.5, -2.0, -3.0, -4.0, -6.0])


def pack_weight(w, fmt):
    k, n = w.shape
    w = f64(np.asarray(w, np.float32).astype(ml_dtypes.bfloat16)).reshape(k // 32, 32, n)
    amax = np.abs(w).max(1)
    if fmt == "e4m3":
        byte = np.frexp(amax)[1] - 1 + 127 - 7
    else:
        mant, ex = np.frexp(amax / 6.0)
        byte = np.where(mant > 0.5, ex, ex - 1) + 127
    byte = np.clip(np.where(amax > 0, byte, 1), 1, 254)
    scaled = (w * np.exp2(127.0 - byte)[:, None, :]).reshape(k, n).astype(np.float32)
    by_word = np.ascontiguousarray(scaled.reshape(k // 512, 128, 4, n).transpose(0, 1, 3, 2))
    if fmt == "e4m3":
        words = by_word.astype(ml_dtypes.float8_e4m3fn).view(np.uint8)
    else:
        c = by_word.astype(ml_dtypes.float4_e2m1fn).view(np.uint8) & 0xF
        words = (c[..., 0::2] | (c[..., 1::2] << 4)).reshape(k // 512, 128, 2 * n)
    return np.ascontiguousarray(words), np.ascontiguousarray(byte.astype(np.uint8).reshape(k // 512, 16, n))


def unpack_weight(words, scales, fmt):
    g, _, n = scales.shape
    words = np.ascontiguousarray(words).reshape(g, 128, n, -1)
    if fmt == "e4m3":
        vals = words.view(ml_dtypes.float8_e4m3fn).astype(np.float64)
    else:
        nib = np.empty((g, 128, n, 4), np.uint8)
        nib[..., 0::2] = words & 0xF
        nib[..., 1::2] = words >> 4
        vals = E2M1[nib]
    vals = vals * np.repeat(np.exp2(scales.astype(np.float64) - 127.0), 8, axis=1)[..., None]
    return vals.transpose(0, 1, 3, 2).reshape(g * 512, n)


def gelu(v):
    return 0.5 * v * (1.0 + np.tanh(np.sqrt(2.0 / np.pi) * (v + 0.044715 * v**3)))


def striped8(idx):
    return np.concatenate([v.reshape(-1, 16).T for v in idx]).astype(np.uint16)


def unstriped8(offs):
    return np.stack([offs[16 * g:16 * g + 16].T.reshape(-1) for g in range(8)]).astype(np.int64)


def runs(v, idx8):
    k = np.arange(v.shape[0])
    return v[k[:, None], idx8[k % 512 // 64]]


def often(T, S):
    return np.random.permutation(T)[(T * np.random.uniform(0, 1, S) ** 4).astype(np.int64)]


T, S, P, K, H, N = 2048, 1024, 512, 1536, 1024, 768

def setup_inputs():
    n = np.random.standard_normal
    s = mx_kscale(K)[:, None]
    u = mx_kscale(H)[:, None]
    d = {}
    d["tab_words"], d["tab_scales"] = pack_weight(n((K, T)) * s, "e4m3")
    d["offs"] = striped8(np.stack([often(T, S) for _ in range(8)]))
    d["pos1"] = striped(np.random.permutation(S)[:P])
    d["pos2"] = striped(np.random.permutation(S)[:P])
    d["w1"] = (n((K, H)) / K ** 0.5 / s * u.T ** 2).astype(np.float32)
    d["b1"] = (0.5 * n(H) * u[:, 0] ** 2).astype(np.float32)
    d["wf"] = (n((H, N)) / H ** 0.5 / u).astype(np.float32)
    d["bf"] = (0.5 * n(N)).astype(np.float32)
    d["wp_words"], d["wp_scales"] = pack_weight(n((H, N)) / H ** 0.5 / u ** 2, "e2m1")
    return d

def reference(tab_words, tab_scales, offs, pos1, pos2, w1, b1, wf, bf, wp_words, wp_scales):
    v = runs(unpack_weight(tab_words, tab_scales, "e4m3"), unstriped8(offs))
    wp = unpack_weight(wp_words, wp_scales, "e2m1")
    lin = (mxq(f64(w1), 0, "e4m3").T @ v) + f64(b1)[:, None]
    h = np.sqrt(np.abs(lin))
    first = h[:, unstriped(pos1)]
    both = first * h[:, unstriped(pos2)]
    yf = mxq(f64(wf), 0, "e4m3").T @ mxq(first, 0, "e4m3")
    yp = wp.T @ mxq(both, 0, "e4m3")
    return np.maximum(yf + f64(bf)[:, None], yp)

@@ -1,0 +1,314 @@
+from contextlib import ExitStack
+
+import concourse.mybir as mybir
+
+T, S, NPAIR, K, H, N = 2048, 1024, 512, 1536, 1024, 768
+FLOPS = 2 * K * H * S + 2 * 2 * H * N * NPAIR
+
+F32 = mybir.dt.float32
+BF16 = mybir.dt.bfloat16
+I32 = mybir.dt.int32
+U32 = mybir.dt.uint32
+U16 = mybir.dt.uint16
+U8 = mybir.dt.uint8
+FP8X4 = mybir.dt.float8_e4m3fn_x4
+FP4X4 = mybir.dt.float4_e2m1fn_x4
+ACT = mybir.ActivationFunctionType
+ALU = mybir.AluOpType
+
+P = 128
+PACK = 4
+K_PASS = P * PACK
+BANK = 512
+K_PASSES = K // K_PASS
+H_PASSES = H // K_PASS
+N_TILES = N // P
+
+
+def tile_list_dance_notation_transitions_kernel(
+    tc, tab_words, tab_scales, offs, pos1, pos2, w1, b1, wf, bf, wp_words, wp_scales, out
+):
+    nc = tc.nc
+    with ExitStack() as ctx:
+        keep = ctx.enter_context(tc.tile_pool(name="keep", bufs=1))
+        ring = ctx.enter_context(tc.tile_pool(name="ring", bufs=2))
+        psum = ctx.enter_context(tc.psum_pool(name="psum", bufs=1))
+
+        offs_sb = keep.tile([P, S // 16], U16, name="offs_sb")
+        pos1_sb = keep.tile([P, NPAIR // 16], U16, name="pos1_sb")
+        pos2_sb = keep.tile([P, NPAIR // 16], U16, name="pos2_sb")
+
+        scale_rows = keep.tile([P, T], U8, name="scale_rows", align_bytes=64)
+        nc.vector.memset(scale_rows[:].bitcast(I32), 0)
+        wp_plane = keep.tile([P, H_PASSES * N], U8, name="wp_plane", align_bytes=64)
+        nc.vector.memset(wp_plane[:].bitcast(I32), 0)
+        warm = keep.tile([P, 2], F32, name="warm")
+        nc.vector.memset(warm[:, 0:1], 1.0)
+        nc.scalar.activation(warm[:, 1:2], warm[:, 0:1], ACT.Sqrt)
+
+        nc.sync.dma_start(offs_sb[:], offs)
+        for a in range(K_PASSES):
+            for e in range(2):
+                nc.sync.dma_start(
+                    out=scale_rows[4 * a + e : P : 16, :].bitcast(I32),
+                    in_=tab_scales[a, e:16:2, :].bitcast(I32),
+                )
+
+        words = {}
+        w1_raw = {}
+
+        def load_table(a):
+            words[a] = keep.tile([P, T], U32, name="words", tag="wide%d" % a, align_bytes=64)
+            nc.sync.dma_start(
+                out=words[a][:].bitcast(I32),
+                in_=tab_words[a].rearrange("p n i -> p (n i)").bitcast(I32),
+            )
+
+        def load_w1(a, b):
+            w1_raw[a, b] = ring.tile([P, PACK, K_PASS], F32, name="w1raw", tag="w1raw", bufs=4)
+            nc.sync.dma_start(
+                out=w1_raw[a, b][:],
+                in_=w1[a * K_PASS : (a + 1) * K_PASS, b * K_PASS : (b + 1) * K_PASS].rearrange(
+                    "(p j) c -> p j c", j=PACK
+                ),
+            )
+
+        b1_sb = keep.tile([P, H_PASSES, PACK], F32, name="b1_sb")
+        bf_sb = keep.tile([P, N_TILES], F32, name="bf_sb")
+        wf_raw = {}
+        wp_sb = {}
+
+        load_table(0)
+        load_w1(0, 0)
+        load_table(1)
+        load_w1(1, 0)
+        nc.sync.dma_start(out=b1_sb[:], in_=b1.rearrange("(b p t) -> p b t", p=P, t=PACK))
+        nc.sync.dma_start(pos1_sb[:], pos1)
+        nc.sync.dma_start(pos2_sb[:], pos2)
+        load_table(2)
+        load_w1(2, 0)
+        for a in range(K_PASSES):
+            load_w1(a, 1)
+        for b in range(H_PASSES):
+            wf_raw[b] = keep.tile([P, PACK, N], F32, name="wfraw%d" % b)
+            nc.sync.dma_start(
+                out=wf_raw[b][:],
+                in_=wf[b * K_PASS : (b + 1) * K_PASS, :].rearrange("(p j) c -> p j c", j=PACK),
+            )
+        for b in range(H_PASSES):
+            wp_sb[b] = keep.tile([P, 2 * N], U8, name="wp%d" % b, align_bytes=64)
+            nc.sync.dma_start(out=wp_sb[b][:].bitcast(I32), in_=wp_words[b].bitcast(I32))
+        for d in range(4):
+            nc.sync.dma_start(
+                out=wp_plane[32 * d : 32 * d + 4, :].bitcast(I32).rearrange("r (b c) -> r b c", b=H_PASSES),
+                in_=wp_scales[:, 4 * d : 4 * d + 4, :].bitcast(I32).rearrange("b r c -> r b c"),
+            )
+        with nc.allow_non_contiguous_dma(reason="one bias value to a partition"):
+            nc.sync.dma_start(out=bf_sb[:], in_=bf.rearrange("(c p) -> p c", p=P))
+
+        picked_rows = keep.tile([P, S], U8, name="picked_rows", align_bytes=64)
+        v_plane = keep.tile([P, S], U8, name="v_plane", align_bytes=64)
+        nc.vector.tensor_copy(picked_rows[:], scale_rows[:].indirect(offs_sb[:]))
+        nc.vector.tensor_copy(v_plane[:].bitcast(I32), picked_rows[:].bitcast(I32))
+        for e in range(2):
+            nc.gpsimd.dma_start(
+                out=v_plane[2 + e : P - 16 : 4, :].bitcast(I32),
+                in_=picked_rows[16 + e : P : 4, :].bitcast(I32),
+            )
+
+        v_words = {}
+
+        def gather_table(a):
+            v_words[a] = keep.tile([P, S], U32, name="vwords%d" % a, align_bytes=64)
+            nc.vector.tensor_copy(v_words[a][:], words[a][:].indirect(offs_sb[:]))
+
+        w1_bf = {}
+        w1_codes = {}
+        w1_plane = {}
+
+        def cast_w1(a, b, vector_m):
+            w1_bf[a, b] = ring.tile([P, K_PASS * PACK], BF16, name="w1bf", tag="w1bf", bufs=3, align_bytes=64)
+            dst = w1_bf[a, b][:].rearrange("p (t m j) -> p m j t", t=PACK, j=PACK)
+            src = w1_raw[a, b][:].rearrange("p j (m t) -> p m j t", t=PACK)
+            if vector_m > 0:
+                nc.vector.tensor_copy(out=dst[:, 0:vector_m], in_=src[:, 0:vector_m])
+            if vector_m < P:
+                nc.scalar.copy(out=dst[:, vector_m:P], in_=src[:, vector_m:P])
+
+        def quantize_w1(a, b, pieces):
+            w1_codes[a, b] = keep.tile([P, K_PASS], U32, name="w1c%d%d" % (a, b), align_bytes=64)
+            w1_plane[a, b] = keep.tile([P, K_PASS], U8, name="w1s%d%d" % (a, b), align_bytes=64)
+            width = K_PASS // pieces
+            for i in range(pieces):
+                nc.vector.quantize_mx(
+                    out=w1_codes[a, b][:, i * width : (i + 1) * width].bitcast(FP8X4),
+                    scales=w1_plane[a, b][:, i * width : (i + 1) * width],
+                    in_=w1_bf[a, b][:, PACK * i * width : PACK * (i + 1) * width],
+                )
+
+        lin = {}
+
+        def first_pass(a, b, t):
+            for half in range(2):
+                if a == 0:
+                    lin[b, t, half] = psum.tile([P, BANK], F32, name="lin", tag="bank%d" % (2 * t + half))
+                cols = slice(half * BANK, (half + 1) * BANK)
+                nc.tensor.matmul_mx(
+                    out=lin[b, t, half][:],
+                    lhsT=w1_codes[a, b][:, t * P : (t + 1) * P].bitcast(FP8X4),
+                    lhsT_scale=w1_plane[a, b][:, t * P : (t + 1) * P],
+                    rhs=v_words[a][:, cols].bitcast(FP8X4),
+                    rhs_scale=v_plane[4 * a : P, cols],
+                    start=(a == 0),
+                    stop=(a == K_PASSES - 1),
+                )
+
+        h = {}
+
+        def root(b, t):
+            mag = ring.tile([P, S], F32, name="mag", tag="mag", bufs=2)
+            for half in range(2):
+                nc.scalar.activation(
+                    mag[:, half * BANK : (half + 1) * BANK], lin[b, t, half][:], ACT.Abs, bias=b1_sb[:, b, t : t + 1]
+                )
+            h[b, t] = ring.tile([P, S], F32, name="h", tag="h", bufs=4)
+            nc.scalar.activation(h[b, t][:], mag[:], ACT.Sqrt)
+
+        early = {}
+        late = {}
+
+        def pick(b, t):
+            if t == 0:
+                early[b] = keep.tile([P, PACK, NPAIR], F32, name="early%d" % b)
+                late[b] = keep.tile([P, PACK, NPAIR], F32, name="late%d" % b)
+            nc.vector.tensor_copy(early[b][:, t, :], h[b, t][:].indirect(pos1_sb[:]))
+            nc.vector.tensor_copy(late[b][:, t, :], h[b, t][:].indirect(pos2_sb[:]))
+
+        first_bf = {}
+        both_bf = {}
+        woven = "p (c i t) -> p c t i"
+        planes = "p t (c i) -> p c t i"
+
+        def weave_first(b):
+            first_bf[b] = keep.tile([P, NPAIR * PACK], BF16, name="firstbf", tag="wide%d" % (2 * b), align_bytes=64)
+            nc.scalar.copy(out=first_bf[b][:].rearrange(woven, i=4, t=PACK), in_=early[b][:].rearrange(planes, i=4))
+
+        def weave_both(b):
+            both_bf[b] = keep.tile([P, NPAIR * PACK], BF16, name="bothbf", tag="wide%d" % (2 * b + 1), align_bytes=64)
+            nc.vector.tensor_tensor(
+                both_bf[b][:].rearrange(woven, i=4, t=PACK),
+                early[b][:].rearrange(planes, i=4),
+                late[b][:].rearrange(planes, i=4),
+                ALU.mult,
+            )
+
+        codes = {}
+        plane = {}
+
+        def quantize_act(which, b, src):
+            codes[which, b] = keep.tile([P, NPAIR], U32, name="c%s%d" % (which, b), align_bytes=64)
+            plane[which, b] = keep.tile([P, NPAIR], U8, name="s%s%d" % (which, b), align_bytes=64)
+            nc.vector.quantize_mx(out=codes[which, b][:].bitcast(FP8X4), scales=plane[which, b][:], in_=src[:])
+
+        wf_bf = {}
+        wf_codes = {}
+        wf_plane = {}
+        WF_PIECE = 256
+
+        def cast_wf(b, i):
+            wf_bf[b, i] = ring.tile([P, WF_PIECE * PACK], BF16, name="wfbf", tag="wfbf", bufs=4, align_bytes=64)
+            nc.scalar.copy(
+                out=wf_bf[b, i][:].rearrange(woven, i=4, t=PACK),
+                in_=wf_raw[b][:, :, i * WF_PIECE : (i + 1) * WF_PIECE].rearrange(planes, i=4),
+            )
+
+        def quantize_wf(b, i):
+            wf_codes[b, i] = keep.tile([P, WF_PIECE], U32, name="wfc%d%d" % (b, i), align_bytes=64)
+            wf_plane[b, i] = keep.tile([P, WF_PIECE], U8, name="wfs%d%d" % (b, i), align_bytes=64)
+            nc.vector.quantize_mx(out=wf_codes[b, i][:].bitcast(FP8X4), scales=wf_plane[b, i][:], in_=wf_bf[b, i][:])
+
+        yf = {}
+        yp = {}
+
+        def second_pass(c, b):
+            if b == 0:
+                yp[c] = psum.tile([P, BANK], F32, name="yp", tag="bank%d" % (2 * (c % 4)))
+                yf[c] = psum.tile([P, BANK], F32, name="yf", tag="bank%d" % (2 * (c % 4) + 1))
+            nc.tensor.matmul_mx(
+                out=yp[c][:],
+                lhsT=wp_sb[b][:, 2 * c * P : 2 * (c + 1) * P].bitcast(FP4X4),
+                lhsT_scale=wp_plane[:, b * N + c * P : b * N + (c + 1) * P],
+                rhs=codes["both", b][:].bitcast(FP8X4),
+                rhs_scale=plane["both", b][:],
+                start=(b == 0),
+                stop=(b == H_PASSES - 1),
+            )
+            cols = slice((c % 2) * P, (c % 2 + 1) * P)
+            nc.tensor.matmul_mx(
+                out=yf[c][:],
+                lhsT=wf_codes[b, c // 2][:, cols].bitcast(FP8X4),
+                lhsT_scale=wf_plane[b, c // 2][:, cols],
+                rhs=codes["first", b][:].bitcast(FP8X4),
+                rhs_scale=plane["first", b][:],
+                start=(b == 0),
+                stop=(b == H_PASSES - 1),
+            )
+
+        def finish(c):
+            yp_sb = ring.tile([P, NPAIR], F32, name="yp_sb", tag="yp_sb", bufs=3)
+            nc.scalar.copy(out=yp_sb[:], in_=yp[c][:])
+            res = ring.tile([P, NPAIR], F32, name="res", tag="res", bufs=4)
+            nc.vector.scalar_tensor_tensor(res[:], yf[c][:], bf_sb[:, c : c + 1], yp_sb[:], ALU.add, ALU.max)
+            nc.sync.dma_start(out=out[c * P : (c + 1) * P, :], in_=res[:])
+
+        for a in range(K_PASSES):
+            last = a == K_PASSES - 1
+            gather_table(a)
+            cast_w1(a, 0, 80 if last else 0)
+            quantize_w1(a, 0, 4 if last else 1)
+            for t in range(PACK):
+                first_pass(a, 0, t)
+
+        root(0, 0)
+        cast_w1(0, 1, P)
+        quantize_w1(0, 1, 1)
+        root(0, 1)
+        pick(0, 0)
+        cast_w1(1, 1, P)
+        cast_w1(2, 1, 0)
+        quantize_w1(1, 1, 1)
+        pick(0, 1)
+        quantize_w1(2, 1, 1)
+        for t in range(2, PACK):
+            root(0, t)
+            pick(0, t)
+        for t in range(PACK):
+            for a in range(K_PASSES):
+                first_pass(a, 1, t)
+
+        root(1, 0)
+        weave_both(0)
+        weave_first(0)
+        pick(1, 0)
+        quantize_act("both", 0, both_bf[0])
+        quantize_act("first", 0, first_bf[0])
+        for t in range(1, PACK):
+            root(1, t)
+            cast_wf(0, t - 1)
+            pick(1, t)
+            quantize_wf(0, t - 1)
+        for c in range(4):
+            second_pass(c, 0)
+        for i in range(3):
+            cast_wf(1, i)
+        weave_first(1)
+        weave_both(1)
+        for i in range(3):
+            quantize_wf(1, i)
+        quantize_act("both", 1, both_bf[1])
+        quantize_act("first", 1, first_bf[1])
+        for c in range(N_TILES):
+            if c >= 4:
+                second_pass(c, 0)
+            second_pass(c, 1)
+            finish(c)

@@ -38,34 +38,27 @@ def tile_list_dance_notation_transitions_kernel(
         pos1_sb = keep.tile([P, NPAIR // 16], U16, name="pos1_sb")
         pos2_sb = keep.tile([P, NPAIR // 16], U16, name="pos2_sb")
 
-        scale_rows = keep.tile([P, T], U8, name="scale_rows", align_bytes=64)
-        nc.vector.memset(scale_rows[:].bitcast(I32), 0)
-        wp_plane = keep.tile([P, H_PASSES * N], U8, name="wp_plane", align_bytes=64)
-        nc.vector.memset(wp_plane[:].bitcast(I32), 0)
-        warm = keep.tile([P, 2], F32, name="warm")
-        nc.vector.memset(warm[:, 0:1], 1.0)
-        nc.scalar.activation(warm[:, 1:2], warm[:, 0:1], ACT.Sqrt)
+        def slot_tile(slot, shape, dtype, name):
+            return keep.tile(shape, dtype, name=name, tag="slot%d" % slot, align_bytes=64)
 
-        nc.sync.dma_start(offs_sb[:], offs)
-        for a in range(K_PASSES):
-            for e in range(2):
-                nc.sync.dma_start(
-                    out=scale_rows[4 * a + e : P : 16, :].bitcast(I32),
-                    in_=tab_scales[a, e:16:2, :].bitcast(I32),
-                )
+        scale_rows = slot_tile(4, [P, T], U8, "scale_rows")
+        nc.vector.memset(scale_rows[:].bitcast(I32), 0)
+        warm_in = slot_tile(1, [P, 1], F32, "warm_in")
+        warm_out = slot_tile(3, [P, 1], F32, "warm_out")
+        nc.vector.memset(warm_in[:], 1.0)
 
         words = {}
         w1_raw = {}
 
-        def load_table(a):
-            words[a] = keep.tile([P, T], U32, name="words", tag="wide%d" % a, align_bytes=64)
+        def load_table(a, slot):
+            words[a] = slot_tile(slot, [P, T], U32, "words")
             nc.sync.dma_start(
                 out=words[a][:].bitcast(I32),
                 in_=tab_words[a].rearrange("p n i -> p (n i)").bitcast(I32),
             )
 
-        def load_w1(a, b):
-            w1_raw[a, b] = ring.tile([P, PACK, K_PASS], F32, name="w1raw", tag="w1raw", bufs=4)
+        def load_w1(a, b, slot):
+            w1_raw[a, b] = slot_tile(slot, [P, PACK, K_PASS], F32, "w1raw")
             nc.sync.dma_start(
                 out=w1_raw[a, b][:],
                 in_=w1[a * K_PASS : (a + 1) * K_PASS, b * K_PASS : (b + 1) * K_PASS].rearrange(
@@ -73,48 +66,19 @@ def tile_list_dance_notation_transitions_kernel(
                 ),
             )
 
-        b1_sb = keep.tile([P, H_PASSES, PACK], F32, name="b1_sb")
-        bf_sb = keep.tile([P, N_TILES], F32, name="bf_sb")
         wf_raw = {}
         wp_sb = {}
 
-        load_table(0)
-        load_w1(0, 0)
-        load_table(1)
-        load_w1(1, 0)
-        nc.sync.dma_start(out=b1_sb[:], in_=b1.rearrange("(b p t) -> p b t", p=P, t=PACK))
-        nc.sync.dma_start(pos1_sb[:], pos1)
-        nc.sync.dma_start(pos2_sb[:], pos2)
-        load_table(2)
-        load_w1(2, 0)
-        for a in range(K_PASSES):
-            load_w1(a, 1)
-        for b in range(H_PASSES):
-            wf_raw[b] = keep.tile([P, PACK, N], F32, name="wfraw%d" % b)
+        def load_wf(b, slot):
+            wf_raw[b] = slot_tile(slot, [P, PACK, N], F32, "wfraw")
             nc.sync.dma_start(
                 out=wf_raw[b][:],
                 in_=wf[b * K_PASS : (b + 1) * K_PASS, :].rearrange("(p j) c -> p j c", j=PACK),
             )
-        for b in range(H_PASSES):
-            wp_sb[b] = keep.tile([P, 2 * N], U8, name="wp%d" % b, align_bytes=64)
-            nc.sync.dma_start(out=wp_sb[b][:].bitcast(I32), in_=wp_words[b].bitcast(I32))
-        for d in range(4):
-            nc.sync.dma_start(
-                out=wp_plane[32 * d : 32 * d + 4, :].bitcast(I32).rearrange("r (b c) -> r b c", b=H_PASSES),
-                in_=wp_scales[:, 4 * d : 4 * d + 4, :].bitcast(I32).rearrange("b r c -> r b c"),
-            )
-        with nc.allow_non_contiguous_dma(reason="one bias value to a partition"):
-            nc.sync.dma_start(out=bf_sb[:], in_=bf.rearrange("(c p) -> p c", p=P))
 
-        picked_rows = keep.tile([P, S], U8, name="picked_rows", align_bytes=64)
-        v_plane = keep.tile([P, S], U8, name="v_plane", align_bytes=64)
-        nc.vector.tensor_copy(picked_rows[:], scale_rows[:].indirect(offs_sb[:]))
-        nc.vector.tensor_copy(v_plane[:].bitcast(I32), picked_rows[:].bitcast(I32))
-        for e in range(2):
-            nc.gpsimd.dma_start(
-                out=v_plane[2 + e : P - 16 : 4, :].bitcast(I32),
-                in_=picked_rows[16 + e : P : 4, :].bitcast(I32),
-            )
+        def load_wp(b, slot):
+            wp_sb[b] = slot_tile(slot, [P, 2 * N], U8, "wp")
+            nc.sync.dma_start(out=wp_sb[b][:].bitcast(I32), in_=wp_words[b].bitcast(I32))
 
         v_words = {}
 
@@ -127,7 +91,10 @@ def tile_list_dance_notation_transitions_kernel(
         w1_plane = {}
 
         def cast_w1(a, b, vector_m):
-            w1_bf[a, b] = ring.tile([P, K_PASS * PACK], BF16, name="w1bf", tag="w1bf", bufs=3, align_bytes=64)
+            if (a, b) == (0, 0):
+                w1_bf[a, b] = slot_tile(2, [P, K_PASS * PACK], BF16, "w1bf")
+            else:
+                w1_bf[a, b] = ring.tile([P, K_PASS * PACK], BF16, name="w1bf", tag="w1bf", bufs=3, align_bytes=64)
             dst = w1_bf[a, b][:].rearrange("p (t m j) -> p m j t", t=PACK, j=PACK)
             src = w1_raw[a, b][:].rearrange("p j (m t) -> p m j t", t=PACK)
             if vector_m > 0:
@@ -136,8 +103,8 @@ def tile_list_dance_notation_transitions_kernel(
                 nc.scalar.copy(out=dst[:, vector_m:P], in_=src[:, vector_m:P])
 
         def quantize_w1(a, b, pieces):
-            w1_codes[a, b] = keep.tile([P, K_PASS], U32, name="w1c%d%d" % (a, b), align_bytes=64)
-            w1_plane[a, b] = keep.tile([P, K_PASS], U8, name="w1s%d%d" % (a, b), align_bytes=64)
+            w1_codes[a, b] = keep.tile([P, K_PASS], U32, name="w1c", tag="w1c%d%d" % (a, b), align_bytes=64)
+            w1_plane[a, b] = keep.tile([P, K_PASS], U8, name="w1s", tag="w1s%d%d" % (a, b), align_bytes=64)
             width = K_PASS // pieces
             for i in range(pieces):
                 nc.vector.quantize_mx(
@@ -165,14 +132,21 @@ def tile_list_dance_notation_transitions_kernel(
 
         h = {}
 
+        mag = {}
+
+        def work_tile(index, shape, dtype, name):
+            return keep.tile(shape, dtype, name=name, tag="work%d" % index, align_bytes=64)
+
+        def magnitude(b, t, half):
+            if half == 0:
+                mag[b, t] = work_tile(t, [P, S], F32, "mag")
+            nc.scalar.activation(
+                mag[b, t][:, half * BANK : (half + 1) * BANK], lin[b, t, half][:], ACT.Abs, bias=b1_sb[:, b, t : t + 1]
+            )
+
         def root(b, t):
-            mag = ring.tile([P, S], F32, name="mag", tag="mag", bufs=2)
-            for half in range(2):
-                nc.scalar.activation(
-                    mag[:, half * BANK : (half + 1) * BANK], lin[b, t, half][:], ACT.Abs, bias=b1_sb[:, b, t : t + 1]
-                )
             h[b, t] = ring.tile([P, S], F32, name="h", tag="h", bufs=4)
-            nc.scalar.activation(h[b, t][:], mag[:], ACT.Sqrt)
+            nc.scalar.activation(h[b, t][:], mag[b, t][:], ACT.Sqrt)
 
         early = {}
         late = {}
@@ -190,11 +164,11 @@ def tile_list_dance_notation_transitions_kernel(
         planes = "p t (c i) -> p c t i"
 
         def weave_first(b):
-            first_bf[b] = keep.tile([P, NPAIR * PACK], BF16, name="firstbf", tag="wide%d" % (2 * b), align_bytes=64)
+            first_bf[b] = work_tile(1, [P, NPAIR * PACK], BF16, "firstbf")
             nc.scalar.copy(out=first_bf[b][:].rearrange(woven, i=4, t=PACK), in_=early[b][:].rearrange(planes, i=4))
 
         def weave_both(b):
-            both_bf[b] = keep.tile([P, NPAIR * PACK], BF16, name="bothbf", tag="wide%d" % (2 * b + 1), align_bytes=64)
+            both_bf[b] = keep.tile([P, NPAIR * PACK], BF16, name="bothbf%d" % b, align_bytes=64)
             nc.vector.tensor_tensor(
                 both_bf[b][:].rearrange(woven, i=4, t=PACK),
                 early[b][:].rearrange(planes, i=4),
@@ -215,8 +189,11 @@ def tile_list_dance_notation_transitions_kernel(
         wf_plane = {}
         WF_PIECE = 256
 
-        def cast_wf(b, i):
-            wf_bf[b, i] = ring.tile([P, WF_PIECE * PACK], BF16, name="wfbf", tag="wfbf", bufs=4, align_bytes=64)
+        def cast_wf(b, i, work=None):
+            if work is None:
+                wf_bf[b, i] = ring.tile([P, WF_PIECE * PACK], BF16, name="wfbf", tag="wfbf", bufs=3, align_bytes=64)
+            else:
+                wf_bf[b, i] = work_tile(work, [P, WF_PIECE * PACK], BF16, "wfbf")
             nc.scalar.copy(
                 out=wf_bf[b, i][:].rearrange(woven, i=4, t=PACK),
                 in_=wf_raw[b][:, :, i * WF_PIECE : (i + 1) * WF_PIECE].rearrange(planes, i=4),
@@ -257,52 +234,131 @@ def tile_list_dance_notation_transitions_kernel(
         def finish(c):
             yp_sb = ring.tile([P, NPAIR], F32, name="yp_sb", tag="yp_sb", bufs=3)
             nc.scalar.copy(out=yp_sb[:], in_=yp[c][:])
-            res = ring.tile([P, NPAIR], F32, name="res", tag="res", bufs=4)
+            res = ring.tile([P, NPAIR], F32, name="res", tag="res", bufs=N_TILES)
             nc.vector.scalar_tensor_tensor(res[:], yf[c][:], bf_sb[:, c : c + 1], yp_sb[:], ALU.add, ALU.max)
             nc.sync.dma_start(out=out[c * P : (c + 1) * P, :], in_=res[:])
 
+        nc.sync.dma_start(offs_sb[:], offs)
+        nc.sync.dma_start(pos1_sb[:], pos1)
+        nc.sync.dma_start(pos2_sb[:], pos2)
+        load_w1(0, 0, 0)
         for a in range(K_PASSES):
-            last = a == K_PASSES - 1
-            gather_table(a)
-            cast_w1(a, 0, 80 if last else 0)
-            quantize_w1(a, 0, 4 if last else 1)
-            for t in range(PACK):
-                first_pass(a, 0, t)
+            for e in range(2):
+                queue = nc.sync if a == K_PASSES - 1 else nc.scalar
+                queue.dma_start(
+                    out=scale_rows[4 * a + e : P : 16, :].bitcast(I32),
+                    in_=tab_scales[a, e:16:2, :].bitcast(I32),
+                )
+        nc.scalar.activation(warm_out[:], warm_in[:], ACT.Sqrt)
 
+        load_table(0, 1)
+        load_table(1, 3)
+
+        cast_w1(0, 0, 0)
+        picked_rows = keep.tile([P, S], U8, name="picked_rows", align_bytes=64)
+        v_plane = slot_tile(0, [P, S], U8, "v_plane")
+        nc.vector.tensor_copy(picked_rows[:], scale_rows[:].indirect(offs_sb[:]))
+        nc.vector.tensor_copy(v_plane[:].bitcast(I32), picked_rows[:].bitcast(I32))
+        for e in range(2):
+            nc.scalar.dma_start(
+                out=v_plane[2 + e : P - 16 : 4, :].bitcast(I32),
+                in_=picked_rows[16 + e : P : 4, :].bitcast(I32),
+            )
+        b1_sb = keep.tile([P, H_PASSES, PACK], F32, name="b1_sb")
+        nc.gpsimd.dma_start(out=b1_sb[:], in_=b1.rearrange("(b p t) -> p b t", p=P, t=PACK))
+        wp_plane = keep.tile([P, H_PASSES * N], U8, name="wp_plane", align_bytes=64)
+        bf_sb = keep.tile([P, N_TILES], F32, name="bf_sb")
+        nc.gpsimd.memset(wp_plane[:].bitcast(I32), 0)
+        for d in range(4):
+            nc.gpsimd.dma_start(
+                out=wp_plane[32 * d : 32 * d + 4, :].bitcast(I32).rearrange("r (b c) -> r b c", b=H_PASSES),
+                in_=wp_scales[:, 4 * d : 4 * d + 4, :].bitcast(I32).rearrange("b r c -> r b c"),
+            )
+        with nc.allow_non_contiguous_dma(reason="one bias value to a partition"):
+            nc.gpsimd.dma_start(out=bf_sb[:], in_=bf.rearrange("(c p) -> p c", p=P))
+
+        load_w1(1, 0, 4)
+        gather_table(0)
+        load_table(2, 1)
+        quantize_w1(0, 0, 1)
+        load_w1(2, 0, 2)
+        for t in range(PACK):
+            first_pass(0, 0, t)
+        gather_table(1)
+        load_w1(0, 1, 3)
+        cast_w1(1, 0, 0)
+        load_w1(1, 1, 4)
+        quantize_w1(1, 0, 1)
+        for t in range(PACK):
+            first_pass(1, 0, t)
+        gather_table(2)
+        load_w1(2, 1, 1)
+        cast_w1(2, 0, 80)
+        load_wf(0, 2)
+        quantize_w1(2, 0, 4)
+        for t in range(PACK):
+            first_pass(2, 0, t)
+
+        magnitude(0, 0, 0)
+        magnitude(0, 0, 1)
         root(0, 0)
         cast_w1(0, 1, P)
+        load_wf(1, 3)
         quantize_w1(0, 1, 1)
-        root(0, 1)
+        magnitude(0, 1, 0)
         pick(0, 0)
+        magnitude(0, 1, 1)
+        magnitude(0, 2, 0)
+        root(0, 1)
         cast_w1(1, 1, P)
-        cast_w1(2, 1, 0)
-        quantize_w1(1, 1, 1)
+        load_wp(0, 4)
         pick(0, 1)
+        quantize_w1(1, 1, 1)
+        cast_w1(2, 1, 0)
+        load_wp(1, 1)
+        magnitude(0, 2, 1)
+        magnitude(0, 3, 0)
+        root(0, 2)
         quantize_w1(2, 1, 1)
-        for t in range(2, PACK):
-            root(0, t)
-            pick(0, t)
+        pick(0, 2)
+        magnitude(0, 3, 1)
         for t in range(PACK):
             for a in range(K_PASSES):
                 first_pass(a, 1, t)
-
+        magnitude(1, 0, 0)
+        root(0, 3)
+        pick(0, 3)
+        magnitude(1, 0, 1)
+        magnitude(1, 1, 0)
         root(1, 0)
         weave_both(0)
-        weave_first(0)
+        magnitude(1, 1, 1)
+        magnitude(1, 2, 0)
+        root(1, 1)
         pick(1, 0)
         quantize_act("both", 0, both_bf[0])
+        weave_first(0)
+        cast_wf(0, 0, 0)
+        pick(1, 1)
         quantize_act("first", 0, first_bf[0])
-        for t in range(1, PACK):
-            root(1, t)
-            cast_wf(0, t - 1)
-            pick(1, t)
-            quantize_wf(0, t - 1)
-        for c in range(4):
-            second_pass(c, 0)
+        magnitude(1, 2, 1)
+        magnitude(1, 3, 0)
+        root(1, 2)
+        quantize_wf(0, 0)
+        pick(1, 2)
+        magnitude(1, 3, 1)
+        cast_wf(0, 1, 2)
+        root(1, 3)
+        cast_wf(0, 2, 3)
+        quantize_wf(0, 1)
+        pick(1, 3)
         for i in range(3):
             cast_wf(1, i)
-        weave_first(1)
+        quantize_wf(0, 2)
+        for c in range(4):
+            second_pass(c, 0)
         weave_both(1)
+        weave_first(1)
         for i in range(3):
             quantize_wf(1, i)
         quantize_act("both", 1, both_bf[1])

@@ -139,13 +139,13 @@ def tile_list_dance_notation_transitions_kernel(
 
         def magnitude(b, t, half):
             if half == 0:
-                mag[b, t] = work_tile(t, [P, S], F32, "mag")
+                mag[b, t] = work_tile(0 if (b, t) == (0, 1) else t, [P, S], F32, "mag")
             nc.scalar.activation(
                 mag[b, t][:, half * BANK : (half + 1) * BANK], lin[b, t, half][:], ACT.Abs, bias=b1_sb[:, b, t : t + 1]
             )
 
         def root(b, t):
-            h[b, t] = ring.tile([P, S], F32, name="h", tag="h", bufs=4)
+            h[b, t] = keep.tile([P, S], F32, name="h", tag="h%d" % t, align_bytes=64)
             nc.scalar.activation(h[b, t][:], mag[b, t][:], ACT.Sqrt)
 
         early = {}
@@ -164,7 +164,7 @@ def tile_list_dance_notation_transitions_kernel(
         planes = "p t (c i) -> p c t i"
 
         def weave_first(b):
-            first_bf[b] = work_tile(1, [P, NPAIR * PACK], BF16, "firstbf")
+            first_bf[b] = work_tile(3 + b, [P, NPAIR * PACK], BF16, "firstbf")
             nc.scalar.copy(out=first_bf[b][:].rearrange(woven, i=4, t=PACK), in_=early[b][:].rearrange(planes, i=4))
 
         def weave_both(b):
@@ -179,63 +179,64 @@ def tile_list_dance_notation_transitions_kernel(
         codes = {}
         plane = {}
 
-        def quantize_act(which, b, src):
-            codes[which, b] = keep.tile([P, NPAIR], U32, name="c%s%d" % (which, b), align_bytes=64)
+        def quantize_act(which, b, src, dst):
+            codes[which, b] = dst
             plane[which, b] = keep.tile([P, NPAIR], U8, name="s%s%d" % (which, b), align_bytes=64)
-            nc.vector.quantize_mx(out=codes[which, b][:].bitcast(FP8X4), scales=plane[which, b][:], in_=src[:])
+            nc.vector.quantize_mx(out=dst.bitcast(FP8X4), scales=plane[which, b][:], in_=src[:])
 
-        wf_bf = {}
-        wf_codes = {}
-        wf_plane = {}
         WF_PIECE = 256
+        wf_bf = {}
+        wf_codes = [keep.tile([P, N], U32, name="wfc%d" % b, align_bytes=64) for b in range(H_PASSES)]
+        wf_plane = [keep.tile([P, N], U8, name="wfs%d" % b, align_bytes=64) for b in range(H_PASSES)]
 
-        def cast_wf(b, i, work=None):
-            if work is None:
-                wf_bf[b, i] = ring.tile([P, WF_PIECE * PACK], BF16, name="wfbf", tag="wfbf", bufs=3, align_bytes=64)
-            else:
-                wf_bf[b, i] = work_tile(work, [P, WF_PIECE * PACK], BF16, "wfbf")
-            nc.scalar.copy(
-                out=wf_bf[b, i][:].rearrange(woven, i=4, t=PACK),
-                in_=wf_raw[b][:, :, i * WF_PIECE : (i + 1) * WF_PIECE].rearrange(planes, i=4),
+        def cast_wf(b, lo, hi, dst):
+            wf_bf[b, lo] = dst
+            nc.scalar.copy(out=dst.rearrange(woven, i=4, t=PACK), in_=wf_raw[b][:, :, lo:hi].rearrange(planes, i=4))
+
+        def quantize_wf(b, lo, hi):
+            nc.vector.quantize_mx(
+                out=wf_codes[b][:, lo:hi].bitcast(FP8X4), scales=wf_plane[b][:, lo:hi], in_=wf_bf[b, lo]
             )
-
-        def quantize_wf(b, i):
-            wf_codes[b, i] = keep.tile([P, WF_PIECE], U32, name="wfc%d%d" % (b, i), align_bytes=64)
-            wf_plane[b, i] = keep.tile([P, WF_PIECE], U8, name="wfs%d%d" % (b, i), align_bytes=64)
-            nc.vector.quantize_mx(out=wf_codes[b, i][:].bitcast(FP8X4), scales=wf_plane[b, i][:], in_=wf_bf[b, i][:])
 
         yf = {}
         yp = {}
 
-        def second_pass(c, b):
+        def pair_pass(c, b, bank=None):
             if b == 0:
-                yp[c] = psum.tile([P, BANK], F32, name="yp", tag="bank%d" % (2 * (c % 4)))
-                yf[c] = psum.tile([P, BANK], F32, name="yf", tag="bank%d" % (2 * (c % 4) + 1))
+                yp[c] = psum.tile([P, BANK], F32, name="yp", tag="bank%d" % bank)
             nc.tensor.matmul_mx(
                 out=yp[c][:],
                 lhsT=wp_sb[b][:, 2 * c * P : 2 * (c + 1) * P].bitcast(FP4X4),
                 lhsT_scale=wp_plane[:, b * N + c * P : b * N + (c + 1) * P],
-                rhs=codes["both", b][:].bitcast(FP8X4),
+                rhs=codes["both", b].bitcast(FP8X4),
                 rhs_scale=plane["both", b][:],
                 start=(b == 0),
                 stop=(b == H_PASSES - 1),
             )
-            cols = slice((c % 2) * P, (c % 2 + 1) * P)
+
+        def alone_pass(c, b, bank=None):
+            if b == 0:
+                yf[c] = psum.tile([P, BANK], F32, name="yf", tag="bank%d" % bank)
+            cols = slice(c * P, (c + 1) * P)
             nc.tensor.matmul_mx(
                 out=yf[c][:],
-                lhsT=wf_codes[b, c // 2][:, cols].bitcast(FP8X4),
-                lhsT_scale=wf_plane[b, c // 2][:, cols],
-                rhs=codes["first", b][:].bitcast(FP8X4),
+                lhsT=wf_codes[b][:, cols].bitcast(FP8X4),
+                lhsT_scale=wf_plane[b][:, cols],
+                rhs=codes["first", b].bitcast(FP8X4),
                 rhs_scale=plane["first", b][:],
                 start=(b == 0),
                 stop=(b == H_PASSES - 1),
             )
 
+        yp_sb = {}
+
+        def copy_pair(c):
+            yp_sb[c] = keep.tile([P, NPAIR], F32, name="yp_sb%d" % c)
+            nc.scalar.copy(out=yp_sb[c][:], in_=yp[c][:])
+
         def finish(c):
-            yp_sb = ring.tile([P, NPAIR], F32, name="yp_sb", tag="yp_sb", bufs=3)
-            nc.scalar.copy(out=yp_sb[:], in_=yp[c][:])
-            res = ring.tile([P, NPAIR], F32, name="res", tag="res", bufs=N_TILES)
-            nc.vector.scalar_tensor_tensor(res[:], yf[c][:], bf_sb[:, c : c + 1], yp_sb[:], ALU.add, ALU.max)
+            res = keep.tile([P, NPAIR], F32, name="res%d" % c)
+            nc.vector.scalar_tensor_tensor(res[:], yf[c][:], bf_sb[:, c : c + 1], yp_sb[c][:], ALU.add, ALU.max)
             nc.sync.dma_start(out=out[c * P : (c + 1) * P, :], in_=res[:])
 
         nc.sync.dma_start(offs_sb[:], offs)
@@ -255,7 +256,7 @@ def tile_list_dance_notation_transitions_kernel(
         load_table(1, 3)
 
         cast_w1(0, 0, 0)
-        picked_rows = keep.tile([P, S], U8, name="picked_rows", align_bytes=64)
+        picked_rows = keep.tile([P, S], U8, name="picked_rows", tag="picked", align_bytes=64)
         v_plane = slot_tile(0, [P, S], U8, "v_plane")
         nc.vector.tensor_copy(picked_rows[:], scale_rows[:].indirect(offs_sb[:]))
         nc.vector.tensor_copy(v_plane[:].bitcast(I32), picked_rows[:].bitcast(I32))
@@ -264,18 +265,8 @@ def tile_list_dance_notation_transitions_kernel(
                 out=v_plane[2 + e : P - 16 : 4, :].bitcast(I32),
                 in_=picked_rows[16 + e : P : 4, :].bitcast(I32),
             )
-        b1_sb = keep.tile([P, H_PASSES, PACK], F32, name="b1_sb")
-        nc.gpsimd.dma_start(out=b1_sb[:], in_=b1.rearrange("(b p t) -> p b t", p=P, t=PACK))
-        wp_plane = keep.tile([P, H_PASSES * N], U8, name="wp_plane", align_bytes=64)
-        bf_sb = keep.tile([P, N_TILES], F32, name="bf_sb")
-        nc.gpsimd.memset(wp_plane[:].bitcast(I32), 0)
-        for d in range(4):
-            nc.gpsimd.dma_start(
-                out=wp_plane[32 * d : 32 * d + 4, :].bitcast(I32).rearrange("r (b c) -> r b c", b=H_PASSES),
-                in_=wp_scales[:, 4 * d : 4 * d + 4, :].bitcast(I32).rearrange("b r c -> r b c"),
-            )
-        with nc.allow_non_contiguous_dma(reason="one bias value to a partition"):
-            nc.gpsimd.dma_start(out=bf_sb[:], in_=bf.rearrange("(c p) -> p c", p=P))
+        b1_sb = keep.tile([P, H_PASSES, PACK], F32, name="b1_sb", tag="picked", align_bytes=64)
+        nc.scalar.dma_start(out=b1_sb[:], in_=b1.rearrange("(b p t) -> p b t", p=P, t=PACK))
 
         load_w1(1, 0, 4)
         gather_table(0)
@@ -305,66 +296,93 @@ def tile_list_dance_notation_transitions_kernel(
         cast_w1(0, 1, P)
         load_wf(1, 3)
         quantize_w1(0, 1, 1)
-        magnitude(0, 1, 0)
+        cast_w1(1, 1, P)
+        load_wp(0, 4)
+        quantize_w1(1, 1, 1)
         pick(0, 0)
+        magnitude(0, 1, 0)
         magnitude(0, 1, 1)
         magnitude(0, 2, 0)
         root(0, 1)
-        cast_w1(1, 1, P)
-        load_wp(0, 4)
-        pick(0, 1)
-        quantize_w1(1, 1, 1)
-        cast_w1(2, 1, 0)
+        cast_w1(2, 1, 64)
         load_wp(1, 1)
+        pick(0, 1)
+        quantize_w1(2, 1, 1)
         magnitude(0, 2, 1)
         magnitude(0, 3, 0)
         root(0, 2)
-        quantize_w1(2, 1, 1)
         pick(0, 2)
         magnitude(0, 3, 1)
         for t in range(PACK):
             for a in range(K_PASSES):
                 first_pass(a, 1, t)
-        magnitude(1, 0, 0)
+        wp_plane = slot_tile(0, [P, H_PASSES * N], U8, "wp_plane")
+        bf_sb = keep.tile([P, N_TILES], F32, name="bf_sb", tag="w1s01", align_bytes=64)
+        nc.gpsimd.memset(wp_plane[:].bitcast(I32), 0)
+        for d in range(4):
+            nc.sync.dma_start(
+                out=wp_plane[32 * d : 32 * d + 4, :].bitcast(I32).rearrange("r (b c) -> r b c", b=H_PASSES),
+                in_=wp_scales[:, 4 * d : 4 * d + 4, :].bitcast(I32).rearrange("b r c -> r b c"),
+            )
+        with nc.allow_non_contiguous_dma(reason="one bias value to a partition"):
+            nc.sync.dma_start(out=bf_sb[:], in_=bf.rearrange("(c p) -> p c", p=P))
+        stage = [keep.tile([P, WF_PIECE * PACK], BF16, name="wfbf%d" % i, align_bytes=64) for i in range(4)]
+        cast_wf(0, 0, 256, stage[0][:])
         root(0, 3)
         pick(0, 3)
+        magnitude(1, 0, 0)
         magnitude(1, 0, 1)
         magnitude(1, 1, 0)
         root(1, 0)
         weave_both(0)
+        pick(1, 0)
+        quantize_wf(0, 0, 256)
         magnitude(1, 1, 1)
         magnitude(1, 2, 0)
         root(1, 1)
-        pick(1, 0)
-        quantize_act("both", 0, both_bf[0])
-        weave_first(0)
-        cast_wf(0, 0, 0)
         pick(1, 1)
-        quantize_act("first", 0, first_bf[0])
+        cast_wf(0, 256, 512, stage[1][:])
+        quantize_wf(0, 256, 512)
         magnitude(1, 2, 1)
         magnitude(1, 3, 0)
         root(1, 2)
-        quantize_wf(0, 0)
         pick(1, 2)
         magnitude(1, 3, 1)
-        cast_wf(0, 1, 2)
+        cast_wf(0, 512, 768, stage[2][:])
+        cast_wf(1, 0, 256, stage[3][:])
         root(1, 3)
-        cast_wf(0, 2, 3)
-        quantize_wf(0, 1)
+        quantize_wf(0, 512, 768)
+        quantize_wf(1, 0, 256)
         pick(1, 3)
-        for i in range(3):
-            cast_wf(1, i)
-        quantize_wf(0, 2)
+        weave_first(0)
+        codes0 = keep.tile([P, 2 * NPAIR], U32, name="codes0", tag="h3", align_bytes=64)
+        codes1 = keep.tile([P, 2 * NPAIR], U32, name="codes1", align_bytes=64)
+        quantize_act("both", 0, both_bf[0], codes0[:, 0:NPAIR])
+        quantize_act("first", 0, first_bf[0], codes0[:, NPAIR : 2 * NPAIR])
         for c in range(4):
-            second_pass(c, 0)
+            pair_pass(c, 0, 2 * c)
+            alone_pass(c, 0, 2 * c + 1)
+        stage_late = work_tile(2, [P, 512 * PACK], BF16, "wfbf")
+        cast_wf(1, 256, 512, stage_late[:, 0:1024])
         weave_both(1)
         weave_first(1)
-        for i in range(3):
-            quantize_wf(1, i)
-        quantize_act("both", 1, both_bf[1])
-        quantize_act("first", 1, first_bf[1])
+        cast_wf(1, 512, 768, stage_late[:, 1024:2048])
+        quantize_wf(1, 256, 512)
+        quantize_act("both", 1, both_bf[1], codes1[:, 0:NPAIR])
+        quantize_act("first", 1, first_bf[1], codes1[:, NPAIR : 2 * NPAIR])
+        quantize_wf(1, 512, 768)
+        pair_pass(0, 1)
+        copy_pair(0)
+        for c in range(4):
+            if c + 1 < 4:
+                pair_pass(c + 1, 1)
+                copy_pair(c + 1)
+            alone_pass(c, 1)
+        for c in range(4, N_TILES):
+            pair_pass(c, 0, 4 * (c - 4))
+            pair_pass(c, 1)
+            copy_pair(c)
+            alone_pass(c, 0, 4 * (c - 4) + 2)
+            alone_pass(c, 1)
         for c in range(N_TILES):
-            if c >= 4:
-                second_pass(c, 0)
-            second_pass(c, 1)
             finish(c)

@@ -23,6 +23,7 @@ BANK = 512
 K_PASSES = K // K_PASS
 H_PASSES = H // K_PASS
 N_TILES = N // P
+PLANE_ROW = (0, 8, 4)
 
 
 def tile_list_dance_notation_transitions_kernel(
@@ -125,7 +126,7 @@ def tile_list_dance_notation_transitions_kernel(
                     lhsT=w1_codes[a, b][:, t * P : (t + 1) * P].bitcast(FP8X4),
                     lhsT_scale=w1_plane[a, b][:, t * P : (t + 1) * P],
                     rhs=v_words[a][:, cols].bitcast(FP8X4),
-                    rhs_scale=v_plane[4 * a : P, cols],
+                    rhs_scale=v_plane[PLANE_ROW[a] : P, cols],
                     start=(a == 0),
                     stop=(a == K_PASSES - 1),
                 )
@@ -243,17 +244,19 @@ def tile_list_dance_notation_transitions_kernel(
         nc.sync.dma_start(pos1_sb[:], pos1)
         nc.sync.dma_start(pos2_sb[:], pos2)
         load_w1(0, 0, 0)
-        for a in range(K_PASSES):
-            for e in range(2):
-                queue = nc.sync if a == K_PASSES - 1 else nc.scalar
-                queue.dma_start(
-                    out=scale_rows[4 * a + e : P : 16, :].bitcast(I32),
-                    in_=tab_scales[a, e:16:2, :].bitcast(I32),
-                )
+        for e in range(2):
+            nc.scalar.dma_start(
+                out=scale_rows[e:P:8, :].bitcast(I32),
+                in_=tab_scales[0:2, e:16:2, :].bitcast(I32).rearrange("a g t -> g a t"),
+            )
+            nc.scalar.dma_start(
+                out=scale_rows[4 + e : P : 16, :].bitcast(I32),
+                in_=tab_scales[2, e:16:2, :].bitcast(I32),
+            )
         nc.scalar.activation(warm_out[:], warm_in[:], ACT.Sqrt)
 
         load_table(0, 1)
-        load_table(1, 3)
+        load_w1(1, 0, 3)
 
         cast_w1(0, 0, 0)
         picked_rows = keep.tile([P, S], U8, name="picked_rows", tag="picked", align_bytes=64)
@@ -265,26 +268,26 @@ def tile_list_dance_notation_transitions_kernel(
                 out=v_plane[2 + e : P - 16 : 4, :].bitcast(I32),
                 in_=picked_rows[16 + e : P : 4, :].bitcast(I32),
             )
-        b1_sb = keep.tile([P, H_PASSES, PACK], F32, name="b1_sb", tag="picked", align_bytes=64)
-        nc.scalar.dma_start(out=b1_sb[:], in_=b1.rearrange("(b p t) -> p b t", p=P, t=PACK))
+        b1_sb = keep.tile([P, H_PASSES, PACK], F32, name="b1_sb")
+        nc.gpsimd.dma_start(out=b1_sb[:], in_=b1.rearrange("(b p t) -> p b t", p=P, t=PACK))
 
-        load_w1(1, 0, 4)
+        load_table(1, 4)
         gather_table(0)
         load_table(2, 1)
         quantize_w1(0, 0, 1)
         load_w1(2, 0, 2)
         for t in range(PACK):
             first_pass(0, 0, t)
-        gather_table(1)
-        load_w1(0, 1, 3)
         cast_w1(1, 0, 0)
-        load_w1(1, 1, 4)
+        load_w1(0, 1, 3)
         quantize_w1(1, 0, 1)
+        gather_table(1)
+        load_w1(1, 1, 4)
         for t in range(PACK):
             first_pass(1, 0, t)
         gather_table(2)
         load_w1(2, 1, 1)
-        cast_w1(2, 0, 80)
+        cast_w1(2, 0, 56)
         load_wf(0, 2)
         quantize_w1(2, 0, 4)
         for t in range(PACK):

from contextlib import ExitStack

import concourse.mybir as mybir

T, S, NPAIR, K, H, N = 2048, 1024, 512, 1536, 1024, 768
FLOPS = 2 * K * H * S + 2 * 2 * H * N * NPAIR

F32 = mybir.dt.float32
BF16 = mybir.dt.bfloat16
I32 = mybir.dt.int32
U32 = mybir.dt.uint32
U16 = mybir.dt.uint16
U8 = mybir.dt.uint8
FP8X4 = mybir.dt.float8_e4m3fn_x4
FP4X4 = mybir.dt.float4_e2m1fn_x4
ACT = mybir.ActivationFunctionType
ALU = mybir.AluOpType

P = 128
PACK = 4
K_PASS = P * PACK
BANK = 512
K_PASSES = K // K_PASS
H_PASSES = H // K_PASS
N_TILES = N // P
PLANE_ROW = (0, 8, 4)


def tile_list_dance_notation_transitions_kernel(
    tc, tab_words, tab_scales, offs, pos1, pos2, w1, b1, wf, bf, wp_words, wp_scales, out
):
    nc = tc.nc
    with ExitStack() as ctx:
        keep = ctx.enter_context(tc.tile_pool(name="keep", bufs=1))
        ring = ctx.enter_context(tc.tile_pool(name="ring", bufs=2))
        psum = ctx.enter_context(tc.psum_pool(name="psum", bufs=1))

        offs_sb = keep.tile([P, S // 16], U16, name="offs_sb")
        pos1_sb = keep.tile([P, NPAIR // 16], U16, name="pos1_sb")
        pos2_sb = keep.tile([P, NPAIR // 16], U16, name="pos2_sb")

        def slot_tile(slot, shape, dtype, name):
            return keep.tile(shape, dtype, name=name, tag="slot%d" % slot, align_bytes=64)

        scale_rows = slot_tile(4, [P, T], U8, "scale_rows")
        nc.vector.memset(scale_rows[:].bitcast(I32), 0)
        warm_in = slot_tile(1, [P, 1], F32, "warm_in")
        warm_out = slot_tile(3, [P, 1], F32, "warm_out")
        nc.vector.memset(warm_in[:], 1.0)

        words = {}
        w1_raw = {}

        def load_table(a, slot):
            words[a] = slot_tile(slot, [P, T], U32, "words")
            nc.sync.dma_start(
                out=words[a][:].bitcast(I32),
                in_=tab_words[a].rearrange("p n i -> p (n i)").bitcast(I32),
            )

        def load_w1(a, b, slot):
            w1_raw[a, b] = slot_tile(slot, [P, PACK, K_PASS], F32, "w1raw")
            nc.sync.dma_start(
                out=w1_raw[a, b][:],
                in_=w1[a * K_PASS : (a + 1) * K_PASS, b * K_PASS : (b + 1) * K_PASS].rearrange(
                    "(p j) c -> p j c", j=PACK
                ),
            )

        wf_raw = {}
        wp_sb = {}

        def load_wf(b, slot):
            wf_raw[b] = slot_tile(slot, [P, PACK, N], F32, "wfraw")
            nc.sync.dma_start(
                out=wf_raw[b][:],
                in_=wf[b * K_PASS : (b + 1) * K_PASS, :].rearrange("(p j) c -> p j c", j=PACK),
            )

        def load_wp(b, slot):
            wp_sb[b] = slot_tile(slot, [P, 2 * N], U8, "wp")
            nc.sync.dma_start(out=wp_sb[b][:].bitcast(I32), in_=wp_words[b].bitcast(I32))

        v_words = {}

        def gather_table(a):
            v_words[a] = keep.tile([P, S], U32, name="vwords%d" % a, align_bytes=64)
            nc.vector.tensor_copy(v_words[a][:], words[a][:].indirect(offs_sb[:]))

        w1_bf = {}
        w1_codes = {}
        w1_plane = {}

        def cast_w1(a, b, vector_m):
            if (a, b) == (0, 0):
                w1_bf[a, b] = slot_tile(2, [P, K_PASS * PACK], BF16, "w1bf")
            else:
                w1_bf[a, b] = ring.tile([P, K_PASS * PACK], BF16, name="w1bf", tag="w1bf", bufs=3, align_bytes=64)
            dst = w1_bf[a, b][:].rearrange("p (t m j) -> p m j t", t=PACK, j=PACK)
            src = w1_raw[a, b][:].rearrange("p j (m t) -> p m j t", t=PACK)
            if vector_m > 0:
                nc.vector.tensor_copy(out=dst[:, 0:vector_m], in_=src[:, 0:vector_m])
            if vector_m < P:
                nc.scalar.copy(out=dst[:, vector_m:P], in_=src[:, vector_m:P])

        def quantize_w1(a, b, pieces):
            w1_codes[a, b] = keep.tile([P, K_PASS], U32, name="w1c", tag="w1c%d%d" % (a, b), align_bytes=64)
            w1_plane[a, b] = keep.tile([P, K_PASS], U8, name="w1s", tag="w1s%d%d" % (a, b), align_bytes=64)
            width = K_PASS // pieces
            for i in range(pieces):
                nc.vector.quantize_mx(
                    out=w1_codes[a, b][:, i * width : (i + 1) * width].bitcast(FP8X4),
                    scales=w1_plane[a, b][:, i * width : (i + 1) * width],
                    in_=w1_bf[a, b][:, PACK * i * width : PACK * (i + 1) * width],
                )

        lin = {}

        def first_pass(a, b, t):
            for half in range(2):
                if a == 0:
                    lin[b, t, half] = psum.tile([P, BANK], F32, name="lin", tag="bank%d" % (2 * t + half))
                cols = slice(half * BANK, (half + 1) * BANK)
                nc.tensor.matmul_mx(
                    out=lin[b, t, half][:],
                    lhsT=w1_codes[a, b][:, t * P : (t + 1) * P].bitcast(FP8X4),
                    lhsT_scale=w1_plane[a, b][:, t * P : (t + 1) * P],
                    rhs=v_words[a][:, cols].bitcast(FP8X4),
                    rhs_scale=v_plane[PLANE_ROW[a] : P, cols],
                    start=(a == 0),
                    stop=(a == K_PASSES - 1),
                )

        h = {}

        mag = {}

        def work_tile(index, shape, dtype, name):
            return keep.tile(shape, dtype, name=name, tag="work%d" % index, align_bytes=64)

        def magnitude(b, t, half):
            if half == 0:
                mag[b, t] = work_tile(0 if (b, t) == (0, 1) else t, [P, S], F32, "mag")
            nc.scalar.activation(
                mag[b, t][:, half * BANK : (half + 1) * BANK], lin[b, t, half][:], ACT.Abs, bias=b1_sb[:, b, t : t + 1]
            )

        def root(b, t):
            h[b, t] = keep.tile([P, S], F32, name="h", tag="h%d" % t, align_bytes=64)
            nc.scalar.activation(h[b, t][:], mag[b, t][:], ACT.Sqrt)

        early = {}
        late = {}

        def pick(b, t):
            if t == 0:
                early[b] = keep.tile([P, PACK, NPAIR], F32, name="early%d" % b)
                late[b] = keep.tile([P, PACK, NPAIR], F32, name="late%d" % b)
            nc.vector.tensor_copy(early[b][:, t, :], h[b, t][:].indirect(pos1_sb[:]))
            nc.vector.tensor_copy(late[b][:, t, :], h[b, t][:].indirect(pos2_sb[:]))

        first_bf = {}
        both_bf = {}
        woven = "p (c i t) -> p c t i"
        planes = "p t (c i) -> p c t i"

        def weave_first(b):
            first_bf[b] = work_tile(3 + b, [P, NPAIR * PACK], BF16, "firstbf")
            nc.scalar.copy(out=first_bf[b][:].rearrange(woven, i=4, t=PACK), in_=early[b][:].rearrange(planes, i=4))

        def weave_both(b):
            both_bf[b] = keep.tile([P, NPAIR * PACK], BF16, name="bothbf%d" % b, align_bytes=64)
            nc.vector.tensor_tensor(
                both_bf[b][:].rearrange(woven, i=4, t=PACK),
                early[b][:].rearrange(planes, i=4),
                late[b][:].rearrange(planes, i=4),
                ALU.mult,
            )

        codes = {}
        plane = {}

        def quantize_act(which, b, src, dst):
            codes[which, b] = dst
            plane[which, b] = keep.tile([P, NPAIR], U8, name="s%s%d" % (which, b), align_bytes=64)
            nc.vector.quantize_mx(out=dst.bitcast(FP8X4), scales=plane[which, b][:], in_=src[:])

        WF_PIECE = 256
        wf_bf = {}
        wf_codes = [keep.tile([P, N], U32, name="wfc%d" % b, align_bytes=64) for b in range(H_PASSES)]
        wf_plane = [keep.tile([P, N], U8, name="wfs%d" % b, align_bytes=64) for b in range(H_PASSES)]

        def cast_wf(b, lo, hi, dst):
            wf_bf[b, lo] = dst
            nc.scalar.copy(out=dst.rearrange(woven, i=4, t=PACK), in_=wf_raw[b][:, :, lo:hi].rearrange(planes, i=4))

        def quantize_wf(b, lo, hi):
            nc.vector.quantize_mx(
                out=wf_codes[b][:, lo:hi].bitcast(FP8X4), scales=wf_plane[b][:, lo:hi], in_=wf_bf[b, lo]
            )

        yf = {}
        yp = {}

        def pair_pass(c, b, bank=None):
            if b == 0:
                yp[c] = psum.tile([P, BANK], F32, name="yp", tag="bank%d" % bank)
            nc.tensor.matmul_mx(
                out=yp[c][:],
                lhsT=wp_sb[b][:, 2 * c * P : 2 * (c + 1) * P].bitcast(FP4X4),
                lhsT_scale=wp_plane[:, b * N + c * P : b * N + (c + 1) * P],
                rhs=codes["both", b].bitcast(FP8X4),
                rhs_scale=plane["both", b][:],
                start=(b == 0),
                stop=(b == H_PASSES - 1),
            )

        def alone_pass(c, b, bank=None):
            if b == 0:
                yf[c] = psum.tile([P, BANK], F32, name="yf", tag="bank%d" % bank)
            cols = slice(c * P, (c + 1) * P)
            nc.tensor.matmul_mx(
                out=yf[c][:],
                lhsT=wf_codes[b][:, cols].bitcast(FP8X4),
                lhsT_scale=wf_plane[b][:, cols],
                rhs=codes["first", b].bitcast(FP8X4),
                rhs_scale=plane["first", b][:],
                start=(b == 0),
                stop=(b == H_PASSES - 1),
            )

        yp_sb = {}

        def copy_pair(c):
            yp_sb[c] = keep.tile([P, NPAIR], F32, name="yp_sb%d" % c)
            nc.scalar.copy(out=yp_sb[c][:], in_=yp[c][:])

        def finish(c):
            res = keep.tile([P, NPAIR], F32, name="res%d" % c)
            nc.vector.scalar_tensor_tensor(res[:], yf[c][:], bf_sb[:, c : c + 1], yp_sb[c][:], ALU.add, ALU.max)
            nc.sync.dma_start(out=out[c * P : (c + 1) * P, :], in_=res[:])

        nc.sync.dma_start(offs_sb[:], offs)
        nc.sync.dma_start(pos1_sb[:], pos1)
        nc.sync.dma_start(pos2_sb[:], pos2)
        load_w1(0, 0, 0)
        for e in range(2):
            nc.scalar.dma_start(
                out=scale_rows[e:P:8, :].bitcast(I32),
                in_=tab_scales[0:2, e:16:2, :].bitcast(I32).rearrange("a g t -> g a t"),
            )
            nc.scalar.dma_start(
                out=scale_rows[4 + e : P : 16, :].bitcast(I32),
                in_=tab_scales[2, e:16:2, :].bitcast(I32),
            )
        nc.scalar.activation(warm_out[:], warm_in[:], ACT.Sqrt)

        load_table(0, 1)
        load_w1(1, 0, 3)

        cast_w1(0, 0, 0)
        picked_rows = keep.tile([P, S], U8, name="picked_rows", tag="picked", align_bytes=64)
        v_plane = slot_tile(0, [P, S], U8, "v_plane")
        nc.vector.tensor_copy(picked_rows[:], scale_rows[:].indirect(offs_sb[:]))
        nc.vector.tensor_copy(v_plane[:].bitcast(I32), picked_rows[:].bitcast(I32))
        for e in range(2):
            nc.scalar.dma_start(
                out=v_plane[2 + e : P - 16 : 4, :].bitcast(I32),
                in_=picked_rows[16 + e : P : 4, :].bitcast(I32),
            )
        b1_sb = keep.tile([P, H_PASSES, PACK], F32, name="b1_sb")
        nc.gpsimd.dma_start(out=b1_sb[:], in_=b1.rearrange("(b p t) -> p b t", p=P, t=PACK))

        load_table(1, 4)
        gather_table(0)
        load_table(2, 1)
        quantize_w1(0, 0, 1)
        load_w1(2, 0, 2)
        for t in range(PACK):
            first_pass(0, 0, t)
        cast_w1(1, 0, 0)
        load_w1(0, 1, 3)
        quantize_w1(1, 0, 1)
        gather_table(1)
        load_w1(1, 1, 4)
        for t in range(PACK):
            first_pass(1, 0, t)
        gather_table(2)
        load_w1(2, 1, 1)
        cast_w1(2, 0, 56)
        load_wf(0, 2)
        quantize_w1(2, 0, 4)
        for t in range(PACK):
            first_pass(2, 0, t)

        magnitude(0, 0, 0)
        magnitude(0, 0, 1)
        root(0, 0)
        cast_w1(0, 1, P)
        load_wf(1, 3)
        quantize_w1(0, 1, 1)
        cast_w1(1, 1, P)
        load_wp(0, 4)
        quantize_w1(1, 1, 1)
        pick(0, 0)
        magnitude(0, 1, 0)
        magnitude(0, 1, 1)
        magnitude(0, 2, 0)
        root(0, 1)
        cast_w1(2, 1, 64)
        load_wp(1, 1)
        pick(0, 1)
        quantize_w1(2, 1, 1)
        magnitude(0, 2, 1)
        magnitude(0, 3, 0)
        root(0, 2)
        pick(0, 2)
        magnitude(0, 3, 1)
        for t in range(PACK):
            for a in range(K_PASSES):
                first_pass(a, 1, t)
        wp_plane = slot_tile(0, [P, H_PASSES * N], U8, "wp_plane")
        bf_sb = keep.tile([P, N_TILES], F32, name="bf_sb", tag="w1s01", align_bytes=64)
        nc.gpsimd.memset(wp_plane[:].bitcast(I32), 0)
        for d in range(4):
            nc.sync.dma_start(
                out=wp_plane[32 * d : 32 * d + 4, :].bitcast(I32).rearrange("r (b c) -> r b c", b=H_PASSES),
                in_=wp_scales[:, 4 * d : 4 * d + 4, :].bitcast(I32).rearrange("b r c -> r b c"),
            )
        with nc.allow_non_contiguous_dma(reason="one bias value to a partition"):
            nc.sync.dma_start(out=bf_sb[:], in_=bf.rearrange("(c p) -> p c", p=P))
        stage = [keep.tile([P, WF_PIECE * PACK], BF16, name="wfbf%d" % i, align_bytes=64) for i in range(4)]
        cast_wf(0, 0, 256, stage[0][:])
        root(0, 3)
        pick(0, 3)
        magnitude(1, 0, 0)
        magnitude(1, 0, 1)
        magnitude(1, 1, 0)
        root(1, 0)
        weave_both(0)
        pick(1, 0)
        quantize_wf(0, 0, 256)
        magnitude(1, 1, 1)
        magnitude(1, 2, 0)
        root(1, 1)
        pick(1, 1)
        cast_wf(0, 256, 512, stage[1][:])
        quantize_wf(0, 256, 512)
        magnitude(1, 2, 1)
        magnitude(1, 3, 0)
        root(1, 2)
        pick(1, 2)
        magnitude(1, 3, 1)
        cast_wf(0, 512, 768, stage[2][:])
        cast_wf(1, 0, 256, stage[3][:])
        root(1, 3)
        quantize_wf(0, 512, 768)
        quantize_wf(1, 0, 256)
        pick(1, 3)
        weave_first(0)
        codes0 = keep.tile([P, 2 * NPAIR], U32, name="codes0", tag="h3", align_bytes=64)
        codes1 = keep.tile([P, 2 * NPAIR], U32, name="codes1", align_bytes=64)
        quantize_act("both", 0, both_bf[0], codes0[:, 0:NPAIR])
        quantize_act("first", 0, first_bf[0], codes0[:, NPAIR : 2 * NPAIR])
        for c in range(4):
            pair_pass(c, 0, 2 * c)
            alone_pass(c, 0, 2 * c + 1)
        stage_late = work_tile(2, [P, 512 * PACK], BF16, "wfbf")
        cast_wf(1, 256, 512, stage_late[:, 0:1024])
        weave_both(1)
        weave_first(1)
        cast_wf(1, 512, 768, stage_late[:, 1024:2048])
        quantize_wf(1, 256, 512)
        quantize_act("both", 1, both_bf[1], codes1[:, 0:NPAIR])
        quantize_act("first", 1, first_bf[1], codes1[:, NPAIR : 2 * NPAIR])
        quantize_wf(1, 512, 768)
        pair_pass(0, 1)
        copy_pair(0)
        for c in range(4):
            if c + 1 < 4:
                pair_pass(c + 1, 1)
                copy_pair(c + 1)
            alone_pass(c, 1)
        for c in range(4, N_TILES):
            pair_pass(c, 0, 4 * (c - 4))
            pair_pass(c, 1)
            copy_pair(c)
            alone_pass(c, 0, 4 * (c - 4) + 2)
            alone_pass(c, 1)
        for c in range(N_TILES):
            finish(c)
